import numpy as np
import ml_dtypes

BF16 = ml_dtypes.bfloat16


def bf(x):
    return np.asarray(x, np.float32).astype(BF16)


def f32(x):
    return np.asarray(x, np.float32)


def f64(x):
    return np.asarray(x).astype(np.float64)


def striped(idx):
    return np.tile(idx.reshape(-1, 16).T, (8, 1))


S, K, M, N, E, Q = 512, 128, 256, 256, 2, 128


def gelu_tanh(v):
    return 0.5 * v * (1.0 + np.tanh(np.sqrt(2.0 / np.pi) * (v + 0.044715 * v**3)))


def setup_inputs():
    return {"base": bf(np.random.standard_normal((M, S))), "x": bf(np.random.standard_normal((K, N))), "w": bf(np.random.standard_normal((E, K, M)) / np.sqrt(K)), "b": f32(0.5 * np.random.standard_normal((M, 1))), "offs": striped(np.random.permutation(S)[:N])}


def reference(base, x, w, b, offs):
    idx = offs[:16].T.reshape(-1)
    z = f64(base).copy()
    for e in range(E):
        z[:, idx[e * Q : (e + 1) * Q]] = f64(w)[e].T @ f64(x)[:, e * Q : (e + 1) * Q]
    return gelu_tanh(z + f64(b))

@@ -1,0 +1,61 @@
+import concourse.mybir as mybir
+from concourse.masks import make_identity
+
+BF16, F32, U16 = mybir.dt.bfloat16, mybir.dt.float32, mybir.dt.uint16
+GELU_TANH = mybir.ActivationFunctionType.Gelu_apprx_tanh
+
+P = 128
+TOKENS = 512
+FEATURES = 256
+ENTRIES = 256
+EXPERTS = 2
+PIECE = ENTRIES // EXPERTS
+PIECE_COLS = PIECE // 16
+BLOCKS = FEATURES // P
+
+FLOPS = 2 * P * FEATURES * ENTRIES
+
+
+def tile_scatter_matmul_kernel(tc, base, x, w, b, offs, out):
+    nc = tc.nc
+    with (
+        tc.tile_pool(name="held", bufs=1) as held,
+        tc.psum_pool(name="banks", bufs=1) as banks,
+    ):
+        offsets = held.tile([P, ENTRIES // 16], U16, name="offsets")
+        nc.sync.dma_start(offsets[:], offs)
+
+        base_rows = [held.tile([P, TOKENS], BF16, name=f"base_rows{a}") for a in range(BLOCKS)]
+        for a in range(BLOCKS):
+            nc.sync.dma_start(base_rows[a][:], base[a * P : (a + 1) * P, :])
+
+        tokens_in = held.tile([P, ENTRIES], BF16, name="tokens_in")
+        nc.scalar.dma_start(tokens_in[:], x)
+        weights = held.tile([P, EXPERTS, FEATURES], BF16, name="weights")
+        nc.scalar.dma_start(weights[:], w.rearrange("e k m -> k e m"))
+
+        bias = held.tile([P, BLOCKS], F32, name="bias")
+        with nc.allow_non_contiguous_dma(reason="one float32 to a partition and block"):
+            nc.scalar.dma_start(bias[:], b.rearrange("(a p) o -> p (a o)", p=P))
+
+        identity = held.tile([P, P], BF16, name="identity")
+        make_identity(nc, identity[:])
+
+        windows = [banks.tile([P, TOKENS], F32, name=f"window{a}") for a in range(BLOCKS)]
+        for a in range(BLOCKS):
+            nc.tensor.matmul(windows[a][:], identity[:], base_rows[a][:], start=True, stop=True)
+
+        for a in range(BLOCKS):
+            for e in range(EXPERTS):
+                nc.tensor.matmul(
+                    windows[a][:].indirect(offsets[:, e * PIECE_COLS : (e + 1) * PIECE_COLS]),
+                    weights[:, e, a * P : (a + 1) * P],
+                    tokens_in[:, e * PIECE : (e + 1) * PIECE],
+                    start=True,
+                    stop=True,
+                )
+
+        for a in range(BLOCKS):
+            result = held.tile([P, TOKENS], F32, name=f"result{a}")
+            nc.scalar.activation(result[:], windows[a][:], GELU_TANH, bias=bias[:, a : a + 1])
+            nc.sync.dma_start(out[a * P : (a + 1) * P, :], result[:])

@@ -12,6 +12,7 @@ EXPERTS = 2
 PIECE = ENTRIES // EXPERTS
 PIECE_COLS = PIECE // 16
 BLOCKS = FEATURES // P
+HALF = TOKENS // 2
 
 FLOPS = 2 * P * FEATURES * ENTRIES
 
@@ -22,21 +23,26 @@ def tile_scatter_matmul_kernel(tc, base, x, w, b, offs, out):
         tc.tile_pool(name="held", bufs=1) as held,
         tc.psum_pool(name="banks", bufs=1) as banks,
     ):
+        base_rows = [held.tile([P, TOKENS], BF16, name=f"base_rows{a}") for a in range(BLOCKS)]
+        nc.sync.dma_start(base_rows[0][:], base[0:P, :])
+        nc.scalar.dma_start(base_rows[1][:], base[P : 2 * P, :])
+
         offsets = held.tile([P, ENTRIES // 16], U16, name="offsets")
         nc.sync.dma_start(offsets[:], offs)
-
-        base_rows = [held.tile([P, TOKENS], BF16, name=f"base_rows{a}") for a in range(BLOCKS)]
-        for a in range(BLOCKS):
-            nc.sync.dma_start(base_rows[a][:], base[a * P : (a + 1) * P, :])
 
         tokens_in = held.tile([P, ENTRIES], BF16, name="tokens_in")
         nc.scalar.dma_start(tokens_in[:], x)
         weights = held.tile([P, EXPERTS, FEATURES], BF16, name="weights")
-        nc.scalar.dma_start(weights[:], w.rearrange("e k m -> k e m"))
+        nc.sync.dma_start(weights[:], w.rearrange("e k m -> k e m"))
 
         bias = held.tile([P, BLOCKS], F32, name="bias")
         with nc.allow_non_contiguous_dma(reason="one float32 to a partition and block"):
             nc.scalar.dma_start(bias[:], b.rearrange("(a p) o -> p (a o)", p=P))
+
+        zeros = held.tile([P, 1], F32, name="zeros")
+        nc.vector.memset(zeros[:], 0.0)
+        unused = held.tile([P, 1], F32, name="unused")
+        nc.scalar.activation(unused[:], zeros[:], GELU_TANH)
 
         identity = held.tile([P, P], BF16, name="identity")
         make_identity(nc, identity[:])
@@ -56,6 +62,10 @@ def tile_scatter_matmul_kernel(tc, base, x, w, b, offs, out):
                 )
 
         for a in range(BLOCKS):
-            result = held.tile([P, TOKENS], F32, name=f"result{a}")
-            nc.scalar.activation(result[:], windows[a][:], GELU_TANH, bias=bias[:, a : a + 1])
-            nc.sync.dma_start(out[a * P : (a + 1) * P, :], result[:])
+            for h in range(2):
+                columns = slice(h * HALF, (h + 1) * HALF)
+                result = held.tile([P, HALF], F32, name=f"result{a}{h}")
+                nc.scalar.activation(
+                    result[:], windows[a][:, columns], GELU_TANH, bias=bias[:, a : a + 1]
+                )
+                nc.sync.dma_start(out[a * P : (a + 1) * P, columns], result[:])

@@ -13,6 +13,8 @@ PIECE = ENTRIES // EXPERTS
 PIECE_COLS = PIECE // 16
 BLOCKS = FEATURES // P
 HALF = TOKENS // 2
+WARM_COLUMNS = 256
+WARM_MATMULS = 2048 // WARM_COLUMNS
 
 FLOPS = 2 * P * FEATURES * ENTRIES
 
@@ -39,10 +41,15 @@ def tile_scatter_matmul_kernel(tc, base, x, w, b, offs, out):
         with nc.allow_non_contiguous_dma(reason="one float32 to a partition and block"):
             nc.scalar.dma_start(bias[:], b.rearrange("(a p) o -> p (a o)", p=P))
 
-        zeros = held.tile([P, 1], F32, name="zeros")
+        zeros = held.tile([P, WARM_COLUMNS], BF16, name="zeros")
         nc.vector.memset(zeros[:], 0.0)
-        unused = held.tile([P, 1], F32, name="unused")
-        nc.scalar.activation(unused[:], zeros[:], GELU_TANH)
+
+        unused_column = held.tile([P, 1], F32, name="unused_column")
+        nc.scalar.activation(unused_column[:], zeros[:, 0:1], GELU_TANH)
+
+        unused_bank = banks.tile([P, WARM_COLUMNS], F32, name="unused_bank")
+        for i in range(WARM_MATMULS):
+            nc.tensor.matmul(unused_bank[:], zeros[:, 0:P], zeros[:], start=True, stop=True)
 
         identity = held.tile([P, P], BF16, name="identity")
         make_identity(nc, identity[:])

@@ -12,9 +12,6 @@ EXPERTS = 2
 PIECE = ENTRIES // EXPERTS
 PIECE_COLS = PIECE // 16
 BLOCKS = FEATURES // P
-HALF = TOKENS // 2
-WARM_COLUMNS = 256
-WARM_MATMULS = 2048 // WARM_COLUMNS
 
 FLOPS = 2 * P * FEATURES * ENTRIES
 
@@ -41,15 +38,10 @@ def tile_scatter_matmul_kernel(tc, base, x, w, b, offs, out):
         with nc.allow_non_contiguous_dma(reason="one float32 to a partition and block"):
             nc.scalar.dma_start(bias[:], b.rearrange("(a p) o -> p (a o)", p=P))
 
-        zeros = held.tile([P, WARM_COLUMNS], BF16, name="zeros")
+        zeros = held.tile([P, 1], F32, name="zeros")
         nc.vector.memset(zeros[:], 0.0)
-
-        unused_column = held.tile([P, 1], F32, name="unused_column")
-        nc.scalar.activation(unused_column[:], zeros[:, 0:1], GELU_TANH)
-
-        unused_bank = banks.tile([P, WARM_COLUMNS], F32, name="unused_bank")
-        for i in range(WARM_MATMULS):
-            nc.tensor.matmul(unused_bank[:], zeros[:, 0:P], zeros[:], start=True, stop=True)
+        unused = held.tile([P, 1], F32, name="unused")
+        nc.scalar.activation(unused[:], zeros[:], GELU_TANH)
 
         identity = held.tile([P, P], BF16, name="identity")
         make_identity(nc, identity[:])
@@ -69,10 +61,6 @@ def tile_scatter_matmul_kernel(tc, base, x, w, b, offs, out):
                 )
 
         for a in range(BLOCKS):
-            for h in range(2):
-                columns = slice(h * HALF, (h + 1) * HALF)
-                result = held.tile([P, HALF], F32, name=f"result{a}{h}")
-                nc.scalar.activation(
-                    result[:], windows[a][:, columns], GELU_TANH, bias=bias[:, a : a + 1]
-                )
-                nc.sync.dma_start(out[a * P : (a + 1) * P, columns], result[:])
+            result = held.tile([P, TOKENS], F32, name=f"result{a}")
+            nc.scalar.activation(result[:], windows[a][:], GELU_TANH, bias=bias[:, a : a + 1])
+            nc.sync.dma_start(out[a * P : (a + 1) * P, :], result[:])

@@ -60,7 +60,8 @@ def tile_scatter_matmul_kernel(tc, base, x, w, b, offs, out):
                     stop=True,
                 )
 
+        store_queues = [nc.sync, nc.scalar]
         for a in range(BLOCKS):
             result = held.tile([P, TOKENS], F32, name=f"result{a}")
             nc.scalar.activation(result[:], windows[a][:], GELU_TANH, bias=bias[:, a : a + 1])
-            nc.sync.dma_start(out[a * P : (a + 1) * P, :], result[:])
+            store_queues[a].dma_start(out[a * P : (a + 1) * P, :], result[:])

@@ -13,6 +13,8 @@ PIECE = ENTRIES // EXPERTS
 PIECE_COLS = PIECE // 16
 BLOCKS = FEATURES // P
 
+WARM_MATMULS = 3
+
 FLOPS = 2 * P * FEATURES * ENTRIES
 
 
@@ -37,6 +39,12 @@ def tile_scatter_matmul_kernel(tc, base, x, w, b, offs, out):
         bias = held.tile([P, BLOCKS], F32, name="bias")
         with nc.allow_non_contiguous_dma(reason="one float32 to a partition and block"):
             nc.scalar.dma_start(bias[:], b.rearrange("(a p) o -> p (a o)", p=P))
+
+        warm_zeros = held.tile([P, TOKENS], BF16, name="warm_zeros")
+        nc.vector.memset(warm_zeros[:], 0.0)
+        spare = banks.tile([P, TOKENS], F32, name="spare")
+        for i in range(WARM_MATMULS):
+            nc.tensor.matmul(spare[:], warm_zeros[:, 0:P], warm_zeros[:], start=True, stop=True)
 
         zeros = held.tile([P, 1], F32, name="zeros")
         nc.vector.memset(zeros[:], 0.0)

@@ -13,7 +13,7 @@ PIECE = ENTRIES // EXPERTS
 PIECE_COLS = PIECE // 16
 BLOCKS = FEATURES // P
 
-WARM_MATMULS = 3
+WARM_MATMULS = 10
 
 FLOPS = 2 * P * FEATURES * ENTRIES
 
@@ -40,11 +40,11 @@ def tile_scatter_matmul_kernel(tc, base, x, w, b, offs, out):
         with nc.allow_non_contiguous_dma(reason="one float32 to a partition and block"):
             nc.scalar.dma_start(bias[:], b.rearrange("(a p) o -> p (a o)", p=P))
 
-        warm_zeros = held.tile([P, TOKENS], BF16, name="warm_zeros")
+        warm_zeros = held.tile([P, P], BF16, name="warm_zeros")
         nc.vector.memset(warm_zeros[:], 0.0)
-        spare = banks.tile([P, TOKENS], F32, name="spare")
+        spare = banks.tile([P, P], F32, name="spare")
         for i in range(WARM_MATMULS):
-            nc.tensor.matmul(spare[:], warm_zeros[:, 0:P], warm_zeros[:], start=True, stop=True)
+            nc.tensor.matmul(spare[:], warm_zeros[:], warm_zeros[:], start=True, stop=True)
 
         zeros = held.tile([P, 1], F32, name="zeros")
         nc.vector.memset(zeros[:], 0.0)

@@ -12,6 +12,7 @@ EXPERTS = 2
 PIECE = ENTRIES // EXPERTS
 PIECE_COLS = PIECE // 16
 BLOCKS = FEATURES // P
+ALIGN = 256
 
 WARM_MATMULS = 10
 
@@ -24,23 +25,23 @@ def tile_scatter_matmul_kernel(tc, base, x, w, b, offs, out):
         tc.tile_pool(name="held", bufs=1) as held,
         tc.psum_pool(name="banks", bufs=1) as banks,
     ):
-        base_rows = [held.tile([P, TOKENS], BF16, name=f"base_rows{a}") for a in range(BLOCKS)]
+        base_rows = [held.tile([P, TOKENS], BF16, name=f"base_rows{a}", align_bytes=ALIGN) for a in range(BLOCKS)]
         nc.sync.dma_start(base_rows[0][:], base[0:P, :])
         nc.scalar.dma_start(base_rows[1][:], base[P : 2 * P, :])
 
         offsets = held.tile([P, ENTRIES // 16], U16, name="offsets")
         nc.sync.dma_start(offsets[:], offs)
 
-        tokens_in = held.tile([P, ENTRIES], BF16, name="tokens_in")
+        tokens_in = held.tile([P, ENTRIES], BF16, name="tokens_in", align_bytes=ALIGN)
         nc.scalar.dma_start(tokens_in[:], x)
-        weights = held.tile([P, EXPERTS, FEATURES], BF16, name="weights")
+        weights = held.tile([P, EXPERTS, FEATURES], BF16, name="weights", align_bytes=ALIGN)
         nc.sync.dma_start(weights[:], w.rearrange("e k m -> k e m"))
 
         bias = held.tile([P, BLOCKS], F32, name="bias")
         with nc.allow_non_contiguous_dma(reason="one float32 to a partition and block"):
             nc.scalar.dma_start(bias[:], b.rearrange("(a p) o -> p (a o)", p=P))
 
-        warm_zeros = held.tile([P, P], BF16, name="warm_zeros")
+        warm_zeros = held.tile([P, P], BF16, name="warm_zeros", align_bytes=ALIGN)
         nc.vector.memset(warm_zeros[:], 0.0)
         spare = banks.tile([P, P], F32, name="spare")
         for i in range(WARM_MATMULS):
@@ -51,7 +52,7 @@ def tile_scatter_matmul_kernel(tc, base, x, w, b, offs, out):
         unused = held.tile([P, 1], F32, name="unused")
         nc.scalar.activation(unused[:], zeros[:], GELU_TANH)
 
-        identity = held.tile([P, P], BF16, name="identity")
+        identity = held.tile([P, P], BF16, name="identity", align_bytes=ALIGN)
         make_identity(nc, identity[:])
 
         windows = [banks.tile([P, TOKENS], F32, name=f"window{a}") for a in range(BLOCKS)]
@@ -70,6 +71,6 @@ def tile_scatter_matmul_kernel(tc, base, x, w, b, offs, out):
 
         store_queues = [nc.sync, nc.scalar]
         for a in range(BLOCKS):
-            result = held.tile([P, TOKENS], F32, name=f"result{a}")
+            result = held.tile([P, TOKENS], F32, name=f"result{a}", align_bytes=ALIGN)
             nc.scalar.activation(result[:], windows[a][:], GELU_TANH, bias=bias[:, a : a + 1])
             store_queues[a].dma_start(out[a * P : (a + 1) * P, :], result[:])

@@ -12,7 +12,7 @@ EXPERTS = 2
 PIECE = ENTRIES // EXPERTS
 PIECE_COLS = PIECE // 16
 BLOCKS = FEATURES // P
-ALIGN = 256
+BF16_BYTES, F32_BYTES = 2, 4
 
 WARM_MATMULS = 10
 
@@ -25,23 +25,23 @@ def tile_scatter_matmul_kernel(tc, base, x, w, b, offs, out):
         tc.tile_pool(name="held", bufs=1) as held,
         tc.psum_pool(name="banks", bufs=1) as banks,
     ):
-        base_rows = [held.tile([P, TOKENS], BF16, name=f"base_rows{a}", align_bytes=ALIGN) for a in range(BLOCKS)]
+        base_rows = [held.tile([P, TOKENS], BF16, name=f"base_rows{a}", align_bytes=TOKENS * BF16_BYTES) for a in range(BLOCKS)]
         nc.sync.dma_start(base_rows[0][:], base[0:P, :])
         nc.scalar.dma_start(base_rows[1][:], base[P : 2 * P, :])
 
         offsets = held.tile([P, ENTRIES // 16], U16, name="offsets")
         nc.sync.dma_start(offsets[:], offs)
 
-        tokens_in = held.tile([P, ENTRIES], BF16, name="tokens_in", align_bytes=ALIGN)
+        tokens_in = held.tile([P, ENTRIES], BF16, name="tokens_in", align_bytes=ENTRIES * BF16_BYTES)
         nc.scalar.dma_start(tokens_in[:], x)
-        weights = held.tile([P, EXPERTS, FEATURES], BF16, name="weights", align_bytes=ALIGN)
+        weights = held.tile([P, EXPERTS, FEATURES], BF16, name="weights", align_bytes=EXPERTS * FEATURES * BF16_BYTES)
         nc.sync.dma_start(weights[:], w.rearrange("e k m -> k e m"))
 
         bias = held.tile([P, BLOCKS], F32, name="bias")
         with nc.allow_non_contiguous_dma(reason="one float32 to a partition and block"):
             nc.scalar.dma_start(bias[:], b.rearrange("(a p) o -> p (a o)", p=P))
 
-        warm_zeros = held.tile([P, P], BF16, name="warm_zeros", align_bytes=ALIGN)
+        warm_zeros = held.tile([P, P], BF16, name="warm_zeros", align_bytes=P * BF16_BYTES)
         nc.vector.memset(warm_zeros[:], 0.0)
         spare = banks.tile([P, P], F32, name="spare")
         for i in range(WARM_MATMULS):
@@ -52,7 +52,7 @@ def tile_scatter_matmul_kernel(tc, base, x, w, b, offs, out):
         unused = held.tile([P, 1], F32, name="unused")
         nc.scalar.activation(unused[:], zeros[:], GELU_TANH)
 
-        identity = held.tile([P, P], BF16, name="identity", align_bytes=ALIGN)
+        identity = held.tile([P, P], BF16, name="identity", align_bytes=P * BF16_BYTES)
         make_identity(nc, identity[:])
 
         windows = [banks.tile([P, TOKENS], F32, name=f"window{a}") for a in range(BLOCKS)]
@@ -71,6 +71,6 @@ def tile_scatter_matmul_kernel(tc, base, x, w, b, offs, out):
 
         store_queues = [nc.sync, nc.scalar]
         for a in range(BLOCKS):
-            result = held.tile([P, TOKENS], F32, name=f"result{a}", align_bytes=ALIGN)
+            result = held.tile([P, TOKENS], F32, name=f"result{a}", align_bytes=TOKENS * F32_BYTES)
             nc.scalar.activation(result[:], windows[a][:], GELU_TANH, bias=bias[:, a : a + 1])
             store_queues[a].dma_start(out[a * P : (a + 1) * P, :], result[:])

import concourse.mybir as mybir
from concourse.masks import make_identity

BF16, F32, U16 = mybir.dt.bfloat16, mybir.dt.float32, mybir.dt.uint16
GELU_TANH = mybir.ActivationFunctionType.Gelu_apprx_tanh

P = 128
TOKENS = 512
FEATURES = 256
ENTRIES = 256
EXPERTS = 2
PIECE = ENTRIES // EXPERTS
PIECE_COLS = PIECE // 16
BLOCKS = FEATURES // P
BF16_BYTES, F32_BYTES = 2, 4

WARM_MATMULS = 10

FLOPS = 2 * P * FEATURES * ENTRIES


def tile_scatter_matmul_kernel(tc, base, x, w, b, offs, out):
    nc = tc.nc
    with (
        tc.tile_pool(name="held", bufs=1) as held,
        tc.psum_pool(name="banks", bufs=1) as banks,
    ):
        base_rows = [held.tile([P, TOKENS], BF16, name=f"base_rows{a}", align_bytes=TOKENS * BF16_BYTES) for a in range(BLOCKS)]
        nc.sync.dma_start(base_rows[0][:], base[0:P, :])
        nc.scalar.dma_start(base_rows[1][:], base[P : 2 * P, :])

        offsets = held.tile([P, ENTRIES // 16], U16, name="offsets")
        nc.sync.dma_start(offsets[:], offs)

        tokens_in = held.tile([P, ENTRIES], BF16, name="tokens_in", align_bytes=ENTRIES * BF16_BYTES)
        nc.scalar.dma_start(tokens_in[:], x)
        weights = held.tile([P, EXPERTS, FEATURES], BF16, name="weights", align_bytes=EXPERTS * FEATURES * BF16_BYTES)
        nc.sync.dma_start(weights[:], w.rearrange("e k m -> k e m"))

        bias = held.tile([P, BLOCKS], F32, name="bias")
        with nc.allow_non_contiguous_dma(reason="one float32 to a partition and block"):
            nc.scalar.dma_start(bias[:], b.rearrange("(a p) o -> p (a o)", p=P))

        warm_zeros = held.tile([P, P], BF16, name="warm_zeros", align_bytes=P * BF16_BYTES)
        nc.vector.memset(warm_zeros[:], 0.0)
        spare = banks.tile([P, P], F32, name="spare")
        for i in range(WARM_MATMULS):
            nc.tensor.matmul(spare[:], warm_zeros[:], warm_zeros[:], start=True, stop=True)

        zeros = held.tile([P, 1], F32, name="zeros")
        nc.vector.memset(zeros[:], 0.0)
        unused = held.tile([P, 1], F32, name="unused")
        nc.scalar.activation(unused[:], zeros[:], GELU_TANH)

        identity = held.tile([P, P], BF16, name="identity", align_bytes=P * BF16_BYTES)
        make_identity(nc, identity[:])

        windows = [banks.tile([P, TOKENS], F32, name=f"window{a}") for a in range(BLOCKS)]
        for a in range(BLOCKS):
            nc.tensor.matmul(windows[a][:], identity[:], base_rows[a][:], start=True, stop=True)

        for a in range(BLOCKS):
            for e in range(EXPERTS):
                nc.tensor.matmul(
                    windows[a][:].indirect(offsets[:, e * PIECE_COLS : (e + 1) * PIECE_COLS]),
                    weights[:, e, a * P : (a + 1) * P],
                    tokens_in[:, e * PIECE : (e + 1) * PIECE],
                    start=True,
                    stop=True,
                )

        store_queues = [nc.sync, nc.scalar]
        for a in range(BLOCKS):
            result = held.tile([P, TOKENS], F32, name=f"result{a}", align_bytes=TOKENS * F32_BYTES)
            nc.scalar.activation(result[:], windows[a][:], GELU_TANH, bias=bias[:, a : a + 1])
            store_queues[a].dma_start(out[a * P : (a + 1) * P, :], result[:])
